import numpy as np, ml_dtypes
CORES = [24,48,72,152,176,200]
N = 6
TK = 64
def setup_inputs(rng):
    rt = (0.75 * rng.standard_normal((128, 1), dtype=np.float32) + rng.standard_normal((128, N), dtype=np.float32) / 2).astype(ml_dtypes.bfloat16)
    return {"x": rng.standard_normal((N, 128, TK), dtype=np.float32).astype(ml_dtypes.bfloat16), "rt": np.broadcast_to(rt, (N, 128, N)).copy(), "w": rng.standard_normal((N, 128, 128), dtype=np.float32).astype(ml_dtypes.bfloat16)}
def setup_inputs_big(rng):
    d = setup_inputs(rng)
    for k in ("x", "w"): d[k] = (d[k].astype(np.float32) * 1024.0).astype(d[k].dtype)
    return d
def setup_inputs_small(rng):
    d = setup_inputs(rng)
    for k in ("x", "w"): d[k] = (d[k].astype(np.float32) * (1 / 1024.0)).astype(d[k].dtype)
    return d
def reference(x, rt, w):
    X, RT, W = x.astype(np.float64), rt.astype(np.float64), w.astype(np.float64)
    y = np.zeros((N, 128, TK))
    for r in range(N):
        sc = RT[r].T @ X[r]
        g = np.exp(sc - sc.max(axis=0)); g = g / g.sum(axis=0)
        y[r] = sum(g[j] * (W[j].T @ X[r]) for j in range(N))
    return {"y": y.astype(ml_dtypes.bfloat16)}

@@ -1,0 +1,169 @@
+from concourse.bass import DstId, RemoteDMATransfer
+from concourse.mybir import AluOpType, AxisListType, ActivationFunctionType
+
+N, TK, P = 6, 64, 128
+
+SCRATCH = {
+    "wd": ("dram", [P, P], "bfloat16"),
+    "wall": ("sbuf", [P, N * P], "bfloat16"),
+    "xs": ("sbuf", [P, TK], "bfloat16"),
+    "rts": ("sbuf", [P, N], "bfloat16"),
+    "ones": ("sbuf", [P, P], "bfloat16"),
+    "ident": ("sbuf", [P, TK], "bfloat16"),
+    "negm": ("sbuf", [P, 1], "float32"),
+    "ssum": ("sbuf", [P, 1], "float32"),
+    "rinv": ("sbuf", [P, 1], "float32"),
+    "e": ("sbuf", [P, N], "float32"),
+    "dg": ("sbuf", [P, N * TK], "bfloat16"),
+    "xg": ("sbuf", [P, N * TK], "bfloat16"),
+    "ysb": ("sbuf", [P, TK], "bfloat16"),
+    "ps_s": ("psum", [P, 512], "float32"),
+    "ps_g": ("psum", [P, 512], "float32"),
+    "ps_y": ("psum", [P, 512], "float32"),
+}
+SEMAPHORES = ["ld_wd", "ld_ws", "ld_xr", "c_id0", "c_id", "c_ones", "m_s", "v_max", "a_exp", "v_rcp", "v_dg", "m_g", "v_xg",
+              "hop", "sent", "m_y", "v_y", "st_y"] + ["arr%d" % j for j in range(N)]
+
+
+def _bits(mask):
+    return [b for b in range(mask.bit_length()) if (mask >> b) & 1]
+
+
+def _mask(bits):
+    m = 0
+    for b in bits:
+        m |= 1 << b
+    return m
+
+
+def _plan(cores, topo):
+    n = len(cores)
+    direct, load, relay = {}, {}, {}
+    for r in range(n):
+        grp = [q for q in range(n) if q == r or topo.same_plane(cores[r], cores[q])]
+        k = grp.index(r) ^ 1
+        direct[r] = grp[k] if k < len(grp) else None
+        if direct[r] is not None:
+            key = (direct[r], topo.die(cores[r]))
+            load[key] = load.get(key, 0) + 1
+    for r in range(n):
+        c = cores[r]
+        free = [h for h in range(c - topo.CORES_PER_CHIP + 1, c + topo.CORES_PER_CHIP)
+                if h >= 0 and h not in cores and topo.host(h) == topo.host(c) and topo.chip(h) == topo.chip(c)]
+        rest = [q for q in range(n) if q != r and q != direct[r]]
+        rest.sort(key=lambda q: (sum(1 for h in free if topo.may_write(h, cores[q])), q))
+        out = {}
+        for q in rest:
+            kind = topo.same_plane(c, cores[q])
+            h = min([h for h in free if topo.may_write(h, cores[q])],
+                    key=lambda h: (load.get((q, topo.die(h)), 0), out.get((kind, topo.die(h)), 0),
+                                   sum(1 for p in cores if topo.may_write(h, p)), h))
+            free.remove(h)
+            relay[(r, q)] = h
+            load[(q, topo.die(h))] = load.get((q, topo.die(h)), 0) + 1
+            out[(kind, topo.die(h))] = out.get((kind, topo.die(h)), 0) + 1
+    return direct, relay
+
+
+def _slot(T, j):
+    return T.wall[:, j * P:(j + 1) * P]
+
+
+def _helper(g, core, T, topo, r, q):
+    dst = T.cores[q]
+    src_mask = topo.mask(T.cores[r], core)
+    k = sum(1 for key in _plan(T.cores, topo)[1] if key[0] == r)
+    per = 1
+    while per * 2 * k <= len(_bits(src_mask)):
+        per *= 2
+    g.wait_ge(T.sem.hop, per)
+    rid, pid = topo.addr(dst, core)
+    m = topo.mask(core, dst)
+    g.remote_dma(_slot(T, r), T.wd[:], T.sem["arr%d" % r], T.sem.sent, pid, rid, m)
+    g.wait_ge(T.sem.sent, len(_bits(m)))
+
+
+def rank_program(g, core, T, topo):
+    cores = list(T.cores)
+    direct, relay = _plan(cores, topo)
+    rank = T.rank_of(core)
+    if rank is None:
+        for (r, q), h in relay.items():
+            if h == core:
+                _helper(g, core, T, topo, r, q)
+        return
+    S = T.sem
+    H = TK
+
+    g.sync.dma_start(T.wd[:], T.w[:]).then_inc(S.ld_wd, 16)
+    g.scalar.dma_start(T.xs[:], T.x[:]).then_inc(S.ld_xr, 16)
+    g.sync.dma_start(T.rts[:], T.rt[:]).then_inc(S.ld_xr, 16)
+    g.sync.dma_start(_slot(T, rank), T.w[:]).then_inc(S.ld_ws, 16)
+
+    g.vector.memset(T.ident[0:H, :], 1.0).then_inc(S.c_id0, 1)
+    g.vector.memset(T.ones[0:H, :], 1.0).then_inc(S.c_ones, 1)
+    g.wait_ge(S.c_id0, 1)
+    g.affine_select(T.ident[0:H, :], T.ident[0:H, :], [[-1, H]], AluOpType.is_equal, 0.0, 0, 1).then_inc(S.c_id, 1)
+
+    g.wait_ge(S.ld_wd, 16)
+    sent = 0
+    mine = [(q, h) for (r, q), h in sorted(relay.items()) if r == rank]
+    if mine:
+        on = _bits(topo.mask(core, mine[0][1]))
+        per = 1
+        while per * 2 * len(mine) <= len(on):
+            per *= 2
+        trs = []
+        for i, (q, h) in enumerate(mine):
+            rid, pid = topo.addr(h, core)
+            trs.append(RemoteDMATransfer(dst_ids=[DstId(rid=rid, pnc=pid)], dma_engine_mask=_mask(on[i * per:(i + 1) * per]),
+                                         remote_sem=S.hop, src=T.wd[:], dst=T.wd[:]))
+            sent += per
+        g.remote_dma_fused(trs, local_sem=S.sent)
+    if direct[rank] is not None:
+        d = cores[direct[rank]]
+        rid, pid = topo.addr(d, core)
+        m = topo.mask(core, d)
+        g.remote_dma(_slot(T, rank), T.wd[:], S["arr%d" % rank], S.sent, pid, rid, m)
+        sent += len(_bits(m))
+
+    g.tensor.wait_ge(S.ld_xr, 32)
+    g.tensor.matmul(T.ps_s[0:H, 0:N], T.xs[:], T.rts[:], True, True).then_inc(S.m_s, 1)
+    g.vector.wait_ge(S.m_s, 1)
+    g.vector.tensor_reduce(T.negm[0:H, :], T.ps_s[0:H, 0:N], AxisListType.X, AluOpType.max, negate=True).then_inc(S.v_max, 1)
+    g.scalar.wait_ge(S.v_max, 1)
+    g.scalar.activation(T.e[0:H, :], T.ps_s[0:H, 0:N], ActivationFunctionType.Exp, bias=T.negm[0:H, :], scale=1.0,
+                        accum_out=T.ssum[0:H, :]).then_inc(S.a_exp, 1)
+    g.vector.wait_ge(S.a_exp, 1)
+    g.vector.reciprocal(T.rinv[0:H, :], T.ssum[0:H, :]).then_inc(S.v_rcp, 1)
+    g.vector.wait_ge(S.v_rcp, 1)
+    g.vector.wait_ge(S.c_id, 1)
+    for j in range(N):
+        g.vector.tensor_scalar(T.dg[0:H, j * TK:(j + 1) * TK], T.ident[0:H, :], T.e[0:H, j:j + 1], T.rinv[0:H, :],
+                               AluOpType.mult, AluOpType.mult).then_inc(S.v_dg, 1)
+    g.tensor.wait_ge(S.v_dg, N)
+    g.tensor.wait_ge(S.c_ones, 1)
+    g.tensor.matmul(T.ps_g[:, 0:N * TK], T.ones[0:H, :], T.dg[0:H, :], True, True).then_inc(S.m_g, 1)
+    g.vector.wait_ge(S.m_g, 1)
+    g.vector.wait_ge(S.ld_xr, 32)
+    for j in range(N):
+        b = slice(j * TK, (j + 1) * TK)
+        g.vector.tensor_tensor(T.xg[:, b], T.ps_g[:, b], T.xs[:], AluOpType.mult).then_inc(S.v_xg, 1)
+
+    g.tensor.wait_ge(S.v_xg, N)
+    others = [j for j in range(N) if j != rank]
+    others.sort(key=lambda j: (direct[j] != rank, not topo.same_plane(cores[j], core), j))
+    for i, j in enumerate([rank] + others):
+        if j == rank:
+            g.tensor.wait_ge(S.ld_ws, 16)
+        else:
+            src = cores[j] if direct[j] == rank else relay[(j, rank)]
+            g.tensor.wait_ge(S["arr%d" % j], len(_bits(topo.mask(src, core))))
+        mm = g.tensor.matmul(T.ps_y[:, 0:TK], _slot(T, j), T.xg[:, j * TK:(j + 1) * TK], i == 0, i == N - 1)
+    mm.then_inc(S.m_y, 1)
+    g.vector.wait_ge(S.m_y, 1)
+    g.vector.tensor_copy(T.ysb[:], T.ps_y[:, 0:TK]).then_inc(S.v_y, 1)
+    g.sync.wait_ge(S.v_y, 1)
+    g.sync.dma_start(T.y[:], T.ysb[:]).then_inc(S.st_y, 16)
+    g.sync.wait_ge(S.st_y, 16)
+    g.wait_ge(S.sent, sent)

@@ -2,14 +2,14 @@ from concourse.bass import DstId, RemoteDMATransfer
 from concourse.mybir import AluOpType, AxisListType, ActivationFunctionType
 
 N, TK, P = 6, 64, 128
+CW = TK + P
 
 SCRATCH = {
     "wd": ("dram", [P, P], "bfloat16"),
     "wall": ("sbuf", [P, N * P], "bfloat16"),
     "xs": ("sbuf", [P, TK], "bfloat16"),
     "rts": ("sbuf", [P, N], "bfloat16"),
-    "ones": ("sbuf", [P, P], "bfloat16"),
-    "ident": ("sbuf", [P, TK], "bfloat16"),
+    "cst": ("sbuf", [P, CW], "bfloat16"),
     "negm": ("sbuf", [P, 1], "float32"),
     "ssum": ("sbuf", [P, 1], "float32"),
     "rinv": ("sbuf", [P, 1], "float32"),
@@ -21,8 +21,8 @@ SCRATCH = {
     "ps_g": ("psum", [P, 512], "float32"),
     "ps_y": ("psum", [P, 512], "float32"),
 }
-SEMAPHORES = ["ld_wd", "ld_ws", "ld_xr", "c_id0", "c_id", "c_ones", "m_s", "v_max", "a_exp", "v_rcp", "v_dg", "m_g", "v_xg",
-              "hop", "sent", "m_y", "v_y", "st_y"] + ["arr%d" % j for j in range(N)]
+SEMAPHORES = ["ld_wd", "ld_ws", "ld_xr", "c_fill", "c_sel", "c_cst", "m_s", "v_max", "a_exp", "v_rcp", "v_dg", "m_g", "v_xg",
+              "hop", "sent", "sent1", "m_y", "v_y", "st_y"] + ["arr%d" % j for j in range(N)]
 
 
 def _bits(mask):
@@ -65,22 +65,53 @@ def _plan(cores, topo):
     return direct, relay
 
 
+def _team(relay, r, cores, topo):
+    return sorted([(q, h) for (rr, q), h in relay.items() if rr == r],
+                  key=lambda t: (topo.same_plane(cores[r], cores[t[0]]), t[0]))
+
+
+def _per(team, core, topo):
+    on = _bits(topo.mask(core, team[0][1]))
+    per = 1
+    while per * 2 * len(team) <= len(on):
+        per *= 2
+    return on, per
+
+
+def _block(i, k):
+    u = CW // 8
+    return (u * i // k) * 8, (u * (i + 1) // k) * 8
+
+
+def _cmask(h, own, dst, topo):
+    return topo.mask(h, dst) & topo.mask(h, own)
+
+
 def _slot(T, j):
     return T.wall[:, j * P:(j + 1) * P]
 
 
-def _helper(g, core, T, topo, r, q):
-    dst = T.cores[q]
-    src_mask = topo.mask(T.cores[r], core)
-    k = sum(1 for key in _plan(T.cores, topo)[1] if key[0] == r)
-    per = 1
-    while per * 2 * k <= len(_bits(src_mask)):
-        per *= 2
-    g.wait_ge(T.sem.hop, per)
+def _helper(g, core, T, topo, relay, r, q):
+    S = T.sem
+    cores = list(T.cores)
+    own, dst = cores[r], cores[q]
+    team = _team(relay, r, cores, topo)
+    a, b = _block(team.index((q, core)), len(team))
+    g.vector.memset(T.cst[:, a:b], 1.0).then_inc(S.c_fill, 1)
+    g.wait_ge(S.c_fill, 1)
+    if a < TK:
+        e = min(b, TK)
+        g.affine_select(T.cst[:, a:e], T.cst[:, a:e], [[-1, e - a]], AluOpType.is_equal, 0.0, -a, 1).then_inc(S.c_sel, 1)
+        g.wait_ge(S.c_sel, 1)
+    mc = _cmask(core, own, dst, topo)
+    rid, pid = topo.addr(own, core)
+    g.remote_dma(T.cst[:, a:b], T.cst[:, a:b], S.c_cst, S.sent, pid, rid, mc)
+
+    g.wait_ge(S.hop, _per(team, own, topo)[1])
     rid, pid = topo.addr(dst, core)
     m = topo.mask(core, dst)
-    g.remote_dma(_slot(T, r), T.wd[:], T.sem["arr%d" % r], T.sem.sent, pid, rid, m)
-    g.wait_ge(T.sem.sent, len(_bits(m)))
+    g.remote_dma(_slot(T, r), T.wd[:], S["arr%d" % r], S.sent, pid, rid, m)
+    g.wait_ge(S.sent, len(_bits(mc)) + len(_bits(m)))
 
 
 def rank_program(g, core, T, topo):
@@ -90,42 +121,36 @@ def rank_program(g, core, T, topo):
     if rank is None:
         for (r, q), h in relay.items():
             if h == core:
-                _helper(g, core, T, topo, r, q)
+                _helper(g, core, T, topo, relay, r, q)
         return
     S = T.sem
     H = TK
+    ident, ones = T.cst[0:H, 0:TK], T.cst[0:H, TK:CW]
+    team = _team(relay, rank, cores, topo)
+    n_cst = sum(len(_bits(_cmask(h, core, cores[q], topo))) for q, h in team)
 
     g.sync.dma_start(T.wd[:], T.w[:]).then_inc(S.ld_wd, 16)
     g.scalar.dma_start(T.xs[:], T.x[:]).then_inc(S.ld_xr, 16)
     g.sync.dma_start(T.rts[:], T.rt[:]).then_inc(S.ld_xr, 16)
-    g.sync.dma_start(_slot(T, rank), T.w[:]).then_inc(S.ld_ws, 16)
-
-    g.vector.memset(T.ident[0:H, :], 1.0).then_inc(S.c_id0, 1)
-    g.vector.memset(T.ones[0:H, :], 1.0).then_inc(S.c_ones, 1)
-    g.wait_ge(S.c_id0, 1)
-    g.affine_select(T.ident[0:H, :], T.ident[0:H, :], [[-1, H]], AluOpType.is_equal, 0.0, 0, 1).then_inc(S.c_id, 1)
 
     g.wait_ge(S.ld_wd, 16)
+    on, per = _per(team, core, topo)
+    trs = []
+    for i, (q, h) in enumerate(team):
+        rid, pid = topo.addr(h, core)
+        trs.append(RemoteDMATransfer(dst_ids=[DstId(rid=rid, pnc=pid)], dma_engine_mask=_mask(on[i * per:(i + 1) * per]),
+                                     remote_sem=S.hop, src=T.wd[:], dst=T.wd[:]))
+    g.remote_dma_fused(trs, local_sem=S.sent1)
     sent = 0
-    mine = [(q, h) for (r, q), h in sorted(relay.items()) if r == rank]
-    if mine:
-        on = _bits(topo.mask(core, mine[0][1]))
-        per = 1
-        while per * 2 * len(mine) <= len(on):
-            per *= 2
-        trs = []
-        for i, (q, h) in enumerate(mine):
-            rid, pid = topo.addr(h, core)
-            trs.append(RemoteDMATransfer(dst_ids=[DstId(rid=rid, pnc=pid)], dma_engine_mask=_mask(on[i * per:(i + 1) * per]),
-                                         remote_sem=S.hop, src=T.wd[:], dst=T.wd[:]))
-            sent += per
-        g.remote_dma_fused(trs, local_sem=S.sent)
     if direct[rank] is not None:
         d = cores[direct[rank]]
         rid, pid = topo.addr(d, core)
         m = topo.mask(core, d)
         g.remote_dma(_slot(T, rank), T.wd[:], S["arr%d" % rank], S.sent, pid, rid, m)
         sent += len(_bits(m))
+
+    g.sync.wait_ge(S.sent1, per * len(team))
+    g.sync.dma_start(_slot(T, rank), T.w[:]).then_inc(S.ld_ws, 16)
 
     g.tensor.wait_ge(S.ld_xr, 32)
     g.tensor.matmul(T.ps_s[0:H, 0:N], T.xs[:], T.rts[:], True, True).then_inc(S.m_s, 1)
@@ -137,13 +162,13 @@ def rank_program(g, core, T, topo):
     g.vector.wait_ge(S.a_exp, 1)
     g.vector.reciprocal(T.rinv[0:H, :], T.ssum[0:H, :]).then_inc(S.v_rcp, 1)
     g.vector.wait_ge(S.v_rcp, 1)
-    g.vector.wait_ge(S.c_id, 1)
+    g.vector.wait_ge(S.c_cst, n_cst)
     for j in range(N):
-        g.vector.tensor_scalar(T.dg[0:H, j * TK:(j + 1) * TK], T.ident[0:H, :], T.e[0:H, j:j + 1], T.rinv[0:H, :],
+        g.vector.tensor_scalar(T.dg[0:H, j * TK:(j + 1) * TK], ident, T.e[0:H, j:j + 1], T.rinv[0:H, :],
                                AluOpType.mult, AluOpType.mult).then_inc(S.v_dg, 1)
     g.tensor.wait_ge(S.v_dg, N)
-    g.tensor.wait_ge(S.c_ones, 1)
-    g.tensor.matmul(T.ps_g[:, 0:N * TK], T.ones[0:H, :], T.dg[0:H, :], True, True).then_inc(S.m_g, 1)
+    g.tensor.wait_ge(S.c_cst, n_cst)
+    g.tensor.matmul(T.ps_g[:, 0:N * TK], ones, T.dg[0:H, :], True, True).then_inc(S.m_g, 1)
     g.vector.wait_ge(S.m_g, 1)
     g.vector.wait_ge(S.ld_xr, 32)
     for j in range(N):
@@ -166,4 +191,5 @@ def rank_program(g, core, T, topo):
     g.sync.wait_ge(S.v_y, 1)
     g.sync.dma_start(T.y[:], T.ysb[:]).then_inc(S.st_y, 16)
     g.sync.wait_ge(S.st_y, 16)
+    g.wait_ge(S.sent1, per * len(team))
     g.wait_ge(S.sent, sent)

@@ -16,13 +16,16 @@ SCRATCH = {
     "e": ("sbuf", [P, N], "float32"),
     "dg": ("sbuf", [P, N * TK], "bfloat16"),
     "xg": ("sbuf", [P, N * TK], "bfloat16"),
+    "dr": ("sbuf", [P, TK], "bfloat16"),
+    "rb": ("sbuf", [P, TK], "float32"),
     "ysb": ("sbuf", [P, TK], "bfloat16"),
     "ps_s": ("psum", [P, 512], "float32"),
     "ps_g": ("psum", [P, 512], "float32"),
+    "ps_r": ("psum", [P, 512], "float32"),
     "ps_y": ("psum", [P, 512], "float32"),
 }
-SEMAPHORES = ["ld_wd", "ld_ws", "ld_xr", "c_fill", "c_sel", "c_cst", "m_s", "v_max", "a_exp", "v_rcp", "v_dg", "m_g", "v_xg",
-              "hop", "sent", "sent1", "m_y", "v_y", "st_y"] + ["arr%d" % j for j in range(N)]
+SEMAPHORES = ["ld_wd", "ld_ws", "ld_xr", "c_fill", "c_sel", "c_cst", "m_s", "v_max", "a_exp", "v_rcp", "v_dg", "v_dr", "m_g",
+              "m_r", "v_rb", "v_xg", "hop", "sent", "sent1", "m_y", "v_y", "st_y"] + ["arr%d" % j for j in range(N)]
 
 
 def _bits(mask):
@@ -43,9 +46,6 @@ def _plan(cores, topo):
         grp = [q for q in range(n) if q == r or topo.same_plane(cores[r], cores[q])]
         k = grp.index(r) ^ 1
         direct[r] = grp[k] if k < len(grp) else None
-        if direct[r] is not None:
-            key = (direct[r], topo.die(cores[r]))
-            load[key] = load.get(key, 0) + 1
     for r in range(n):
         c = cores[r]
         free = [h for h in range(c - topo.CORES_PER_CHIP + 1, c + topo.CORES_PER_CHIP)
@@ -56,7 +56,7 @@ def _plan(cores, topo):
         for q in rest:
             kind = topo.same_plane(c, cores[q])
             h = min([h for h in free if topo.may_write(h, cores[q])],
-                    key=lambda h: (load.get((q, topo.die(h)), 0), out.get((kind, topo.die(h)), 0),
+                    key=lambda h: (out.get((kind, topo.die(h)), 0), load.get((q, topo.die(h)), 0),
                                    sum(1 for p in cores if topo.may_write(h, p)), h))
             free.remove(h)
             relay[(r, q)] = h
@@ -66,8 +66,12 @@ def _plan(cores, topo):
 
 
 def _team(relay, r, cores, topo):
-    return sorted([(q, h) for (rr, q), h in relay.items() if rr == r],
-                  key=lambda t: (topo.same_plane(cores[r], cores[t[0]]), t[0]))
+    seen, keyed = {}, []
+    for q, h in sorted((q, h) for (rr, q), h in relay.items() if rr == r):
+        k = (topo.same_plane(cores[r], cores[q]), topo.die(h))
+        keyed.append(((k[0], seen.get(k, 0), topo.die(h) == topo.die(cores[r])), (q, h)))
+        seen[k] = seen.get(k, 0) + 1
+    return [t for _, t in sorted(keyed)]
 
 
 def _per(team, core, topo):
@@ -135,10 +139,10 @@ def rank_program(g, core, T, topo):
 
     g.wait_ge(S.ld_wd, 16)
     on, per = _per(team, core, topo)
-    trs = []
+    trs, step = [], len(on) // per
     for i, (q, h) in enumerate(team):
         rid, pid = topo.addr(h, core)
-        trs.append(RemoteDMATransfer(dst_ids=[DstId(rid=rid, pnc=pid)], dma_engine_mask=_mask(on[i * per:(i + 1) * per]),
+        trs.append(RemoteDMATransfer(dst_ids=[DstId(rid=rid, pnc=pid)], dma_engine_mask=_mask(on[i::step]),
                                      remote_sem=S.hop, src=T.wd[:], dst=T.wd[:]))
     g.remote_dma_fused(trs, local_sem=S.sent1)
     sent = 0
@@ -160,20 +164,25 @@ def rank_program(g, core, T, topo):
     g.scalar.activation(T.e[0:H, :], T.ps_s[0:H, 0:N], ActivationFunctionType.Exp, bias=T.negm[0:H, :], scale=1.0,
                         accum_out=T.ssum[0:H, :]).then_inc(S.a_exp, 1)
     g.vector.wait_ge(S.a_exp, 1)
-    g.vector.reciprocal(T.rinv[0:H, :], T.ssum[0:H, :]).then_inc(S.v_rcp, 1)
-    g.vector.wait_ge(S.v_rcp, 1)
     g.vector.wait_ge(S.c_cst, n_cst)
     for j in range(N):
-        g.vector.tensor_scalar(T.dg[0:H, j * TK:(j + 1) * TK], ident, T.e[0:H, j:j + 1], T.rinv[0:H, :],
-                               AluOpType.mult, AluOpType.mult).then_inc(S.v_dg, 1)
+        g.vector.tensor_scalar(T.dg[0:H, j * TK:(j + 1) * TK], ident, T.e[0:H, j:j + 1], None,
+                               AluOpType.mult).then_inc(S.v_dg, 1)
+    g.vector.reciprocal(T.rinv[0:H, :], T.ssum[0:H, :]).then_inc(S.v_rcp, 1)
+    g.vector.wait_ge(S.v_rcp, 1)
+    g.vector.tensor_scalar(T.dr[0:H, :], ident, T.rinv[0:H, :], None, AluOpType.mult).then_inc(S.v_dr, 1)
     g.tensor.wait_ge(S.v_dg, N)
     g.tensor.wait_ge(S.c_cst, n_cst)
     g.tensor.matmul(T.ps_g[:, 0:N * TK], ones, T.dg[0:H, :], True, True).then_inc(S.m_g, 1)
+    g.tensor.wait_ge(S.v_dr, 1)
+    g.tensor.matmul(T.ps_r[:, 0:TK], ones, T.dr[0:H, :], True, True).then_inc(S.m_r, 1)
     g.vector.wait_ge(S.m_g, 1)
     g.vector.wait_ge(S.ld_xr, 32)
     for j in range(N):
         b = slice(j * TK, (j + 1) * TK)
         g.vector.tensor_tensor(T.xg[:, b], T.ps_g[:, b], T.xs[:], AluOpType.mult).then_inc(S.v_xg, 1)
+    g.vector.wait_ge(S.m_r, 1)
+    g.vector.tensor_copy(T.rb[:], T.ps_r[:, 0:TK]).then_inc(S.v_rb, 1)
 
     g.tensor.wait_ge(S.v_xg, N)
     others = [j for j in range(N) if j != rank]
@@ -186,8 +195,9 @@ def rank_program(g, core, T, topo):
             g.tensor.wait_ge(S["arr%d" % j], len(_bits(topo.mask(src, core))))
         mm = g.tensor.matmul(T.ps_y[:, 0:TK], _slot(T, j), T.xg[:, j * TK:(j + 1) * TK], i == 0, i == N - 1)
     mm.then_inc(S.m_y, 1)
+    g.vector.wait_ge(S.v_rb, 1)
     g.vector.wait_ge(S.m_y, 1)
-    g.vector.tensor_copy(T.ysb[:], T.ps_y[:, 0:TK]).then_inc(S.v_y, 1)
+    g.vector.tensor_tensor(T.ysb[:], T.ps_y[:, 0:TK], T.rb[:], AluOpType.mult).then_inc(S.v_y, 1)
     g.sync.wait_ge(S.v_y, 1)
     g.sync.dma_start(T.y[:], T.ysb[:]).then_inc(S.st_y, 16)
     g.sync.wait_ge(S.st_y, 16)

@@ -10,6 +10,8 @@ SCRATCH = {
     "xs": ("sbuf", [P, TK], "bfloat16"),
     "rts": ("sbuf", [P, N], "bfloat16"),
     "cst": ("sbuf", [P, CW], "bfloat16"),
+    "ob": ("sbuf", [P, CW], "bfloat16"),
+    "zb": ("sbuf", [P, CW], "bfloat16"),
     "negm": ("sbuf", [P, 1], "float32"),
     "ssum": ("sbuf", [P, 1], "float32"),
     "rinv": ("sbuf", [P, 1], "float32"),
@@ -24,8 +26,9 @@ SCRATCH = {
     "ps_r": ("psum", [P, 512], "float32"),
     "ps_y": ("psum", [P, 512], "float32"),
 }
-SEMAPHORES = ["ld_wd", "ld_ws", "ld_xr", "c_fill", "c_sel", "c_cst", "m_s", "v_max", "a_exp", "v_rcp", "v_dg", "v_dr", "m_g",
-              "m_r", "v_rb", "v_xg", "hop", "sent", "sent1", "m_y", "v_y", "st_y"] + ["arr%d" % j for j in range(N)]
+SEMAPHORES = ["ld_wd", "ld_ws", "ld_xr", "c_fill", "c_sel", "c_cst", "c_own", "c_zero", "c_peer", "a_one", "m_s", "v_max",
+              "a_exp", "v_rcp", "v_dg", "v_dr", "m_g", "m_r", "v_rb", "v_xg", "hop", "sent", "sent1", "m_y", "v_y",
+              "st_y"] + ["arr%d" % j for j in range(N)]
 
 
 def _bits(mask):
@@ -65,13 +68,36 @@ def _plan(cores, topo):
     return direct, relay
 
 
-def _team(relay, r, cores, topo):
-    seen, keyed = {}, []
-    for q, h in sorted((q, h) for (rr, q), h in relay.items() if rr == r):
-        k = (topo.same_plane(cores[r], cores[q]), topo.die(h))
-        keyed.append(((k[0], seen.get(k, 0), topo.die(h) == topo.die(cores[r])), (q, h)))
-        seen[k] = seen.get(k, 0) + 1
-    return [t for _, t in sorted(keyed)]
+def _teams(relay, cores, topo):
+    state, teams = {}, {}
+    for r in range(len(cores)):
+        own = topo.die(cores[r])
+        mine = sorted((q, h) for (rr, q), h in relay.items() if rr == r)
+        rank_of = {}
+        for t in mine:
+            seen = state.get((t[0], topo.die(t[1])), [])
+            want = 1 if not seen else (2 if any(seen) else 0)
+            rank_of[t] = (want, topo.same_plane(cores[r], cores[t[0]]), topo.die(t[1]) == own, t)
+        ranked = sorted(mine, key=lambda t: rank_of[t])
+        half = (len(mine) + 1) // 2
+        early = []
+        for t in ranked:
+            if len(early) < half and 2 * sum(1 for u in early if topo.die(u[1]) == topo.die(t[1])) < half:
+                early.append(t)
+        for t in ranked:
+            if len(early) < half and t not in early:
+                early.append(t)
+        late = [t for t in mine if t not in early]
+        teams[r] = (sorted(early, key=lambda t: (topo.die(t[1]) == own, rank_of[t]))
+                    + sorted(late, key=lambda t: (topo.die(t[1]) == own, rank_of[t])))
+        for t in mine:
+            state.setdefault((t[0], topo.die(t[1])), []).append(t in early)
+    return teams
+
+
+def _share(direct, teams, r):
+    peers = [p for p in sorted(direct) if direct[p] == r]
+    return teams[r], peers, len(teams[r]) + len(peers) + 1
 
 
 def _per(team, core, topo):
@@ -80,6 +106,16 @@ def _per(team, core, topo):
     while per * 2 * len(team) <= len(on):
         per *= 2
     return on, per
+
+
+def _engines(team, core, far, topo):
+    on, per = _per(team, core, topo)
+    off = 0 if far is None else topo.mask(core, far)
+    on = [b for b in on if (off >> b) & 1] + [b for b in on if not (off >> b) & 1]
+    nh = (len(team) + 1) // 2
+    nl = len(team) - nh
+    a, b = on[:per * nh], on[per * nh:per * len(team)]
+    return [a[i::nh] for i in range(nh)] + [b[i::nl] for i in range(nl)]
 
 
 def _block(i, k):
@@ -95,12 +131,12 @@ def _slot(T, j):
     return T.wall[:, j * P:(j + 1) * P]
 
 
-def _helper(g, core, T, topo, relay, r, q):
+def _helper(g, core, T, topo, direct, teams, r, q):
     S = T.sem
     cores = list(T.cores)
     own, dst = cores[r], cores[q]
-    team = _team(relay, r, cores, topo)
-    a, b = _block(team.index((q, core)), len(team))
+    team, _, k = _share(direct, teams, r)
+    a, b = _block(len(team) - 1 - team.index((q, core)), k)
     g.vector.memset(T.cst[:, a:b], 1.0).then_inc(S.c_fill, 1)
     g.wait_ge(S.c_fill, 1)
     if a < TK:
@@ -121,35 +157,52 @@ def _helper(g, core, T, topo, relay, r, q):
 def rank_program(g, core, T, topo):
     cores = list(T.cores)
     direct, relay = _plan(cores, topo)
+    teams = _teams(relay, cores, topo)
     rank = T.rank_of(core)
     if rank is None:
         for (r, q), h in relay.items():
             if h == core:
-                _helper(g, core, T, topo, relay, r, q)
+                _helper(g, core, T, topo, direct, teams, r, q)
         return
     S = T.sem
     H = TK
     ident, ones = T.cst[0:H, 0:TK], T.cst[0:H, TK:CW]
-    team = _team(relay, rank, cores, topo)
+    team, peers, k = _share(direct, teams, rank)
     n_cst = sum(len(_bits(_cmask(h, core, cores[q], topo))) for q, h in team)
+    n_peer = sum(len(_bits(topo.mask(cores[p], core))) for p in peers)
+    far = direct[rank]
 
     g.sync.dma_start(T.wd[:], T.w[:]).then_inc(S.ld_wd, 16)
     g.scalar.dma_start(T.xs[:], T.x[:]).then_inc(S.ld_xr, 16)
     g.sync.dma_start(T.rts[:], T.rt[:]).then_inc(S.ld_xr, 16)
 
+    sent = 0
+    if far is not None:
+        tq, pq, kq = _share(direct, teams, far)
+        a1, b1 = _block(len(tq) + pq.index(rank), kq)
+        g.vector.memset(T.ob[:, 0:b1 - a1], 1.0).then_inc(S.c_own, 1)
+        g.wait_ge(S.c_own, 1)
+        rid, pid = topo.addr(cores[far], core)
+        m = topo.mask(core, cores[far])
+        g.remote_dma(T.cst[:, a1:b1], T.ob[:, 0:b1 - a1], S.c_peer, S.sent, pid, rid, m)
+        sent += len(_bits(m))
+    a0, b0 = _block(k - 1, k)
+    g.vector.memset(T.zb[0:H, 0:b0 - a0], 0.0).then_inc(S.c_zero, 1)
+    g.scalar.wait_ge(S.c_zero, 1)
+    g.scalar.activation(T.cst[0:H, a0:b0], T.zb[0:H, 0:b0 - a0], ActivationFunctionType.Exp).then_inc(S.a_one, 1)
+
     g.wait_ge(S.ld_wd, 16)
-    on, per = _per(team, core, topo)
-    trs, step = [], len(on) // per
+    per = _per(team, core, topo)[1]
+    eng = _engines(team, core, None if far is None else cores[far], topo)
+    trs = []
     for i, (q, h) in enumerate(team):
         rid, pid = topo.addr(h, core)
-        trs.append(RemoteDMATransfer(dst_ids=[DstId(rid=rid, pnc=pid)], dma_engine_mask=_mask(on[i::step]),
+        trs.append(RemoteDMATransfer(dst_ids=[DstId(rid=rid, pnc=pid)], dma_engine_mask=_mask(eng[i]),
                                      remote_sem=S.hop, src=T.wd[:], dst=T.wd[:]))
     g.remote_dma_fused(trs, local_sem=S.sent1)
-    sent = 0
-    if direct[rank] is not None:
-        d = cores[direct[rank]]
-        rid, pid = topo.addr(d, core)
-        m = topo.mask(core, d)
+    if far is not None:
+        rid, pid = topo.addr(cores[far], core)
+        m = topo.mask(core, cores[far])
         g.remote_dma(_slot(T, rank), T.wd[:], S["arr%d" % rank], S.sent, pid, rid, m)
         sent += len(_bits(m))
 
@@ -173,6 +226,9 @@ def rank_program(g, core, T, topo):
     g.vector.tensor_scalar(T.dr[0:H, :], ident, T.rinv[0:H, :], None, AluOpType.mult).then_inc(S.v_dr, 1)
     g.tensor.wait_ge(S.v_dg, N)
     g.tensor.wait_ge(S.c_cst, n_cst)
+    g.tensor.wait_ge(S.a_one, 1)
+    if n_peer:
+        g.tensor.wait_ge(S.c_peer, n_peer)
     g.tensor.matmul(T.ps_g[:, 0:N * TK], ones, T.dg[0:H, :], True, True).then_inc(S.m_g, 1)
     g.tensor.wait_ge(S.v_dr, 1)
     g.tensor.matmul(T.ps_r[:, 0:TK], ones, T.dr[0:H, :], True, True).then_inc(S.m_r, 1)
@@ -186,7 +242,8 @@ def rank_program(g, core, T, topo):
 
     g.tensor.wait_ge(S.v_xg, N)
     others = [j for j in range(N) if j != rank]
-    others.sort(key=lambda j: (direct[j] != rank, not topo.same_plane(cores[j], core), j))
+    others.sort(key=lambda j: (0, 0, 0, j) if direct[j] == rank else
+                (1, teams[j].index((rank, relay[(j, rank)])), not topo.same_plane(cores[j], core), j))
     for i, j in enumerate([rank] + others):
         if j == rank:
             g.tensor.wait_ge(S.ld_ws, 16)

from concourse.bass import DstId, RemoteDMATransfer
from concourse.mybir import AluOpType, AxisListType, ActivationFunctionType

N, TK, P = 6, 64, 128
CW = TK + P

SCRATCH = {
    "wd": ("dram", [P, P], "bfloat16"),
    "wall": ("sbuf", [P, N * P], "bfloat16"),
    "xs": ("sbuf", [P, TK], "bfloat16"),
    "rts": ("sbuf", [P, N], "bfloat16"),
    "cst": ("sbuf", [P, CW], "bfloat16"),
    "ob": ("sbuf", [P, CW], "bfloat16"),
    "zb": ("sbuf", [P, CW], "bfloat16"),
    "negm": ("sbuf", [P, 1], "float32"),
    "ssum": ("sbuf", [P, 1], "float32"),
    "rinv": ("sbuf", [P, 1], "float32"),
    "e": ("sbuf", [P, N], "float32"),
    "dg": ("sbuf", [P, N * TK], "bfloat16"),
    "xg": ("sbuf", [P, N * TK], "bfloat16"),
    "dr": ("sbuf", [P, TK], "bfloat16"),
    "rb": ("sbuf", [P, TK], "float32"),
    "ysb": ("sbuf", [P, TK], "bfloat16"),
    "ps_s": ("psum", [P, 512], "float32"),
    "ps_g": ("psum", [P, 512], "float32"),
    "ps_r": ("psum", [P, 512], "float32"),
    "ps_y": ("psum", [P, 512], "float32"),
}
SEMAPHORES = ["ld_wd", "ld_ws", "ld_xr", "c_fill", "c_sel", "c_cst", "c_own", "c_zero", "c_peer", "a_one", "m_s", "v_max",
              "a_exp", "v_rcp", "v_dg", "v_dr", "m_g", "m_r", "v_rb", "v_xg", "hop", "sent", "sent1", "m_y", "v_y",
              "st_y"] + ["arr%d" % j for j in range(N)]


def _bits(mask):
    return [b for b in range(mask.bit_length()) if (mask >> b) & 1]


def _mask(bits):
    m = 0
    for b in bits:
        m |= 1 << b
    return m


def _plan(cores, topo):
    n = len(cores)
    direct, load, relay = {}, {}, {}
    for r in range(n):
        grp = [q for q in range(n) if q == r or topo.same_plane(cores[r], cores[q])]
        k = grp.index(r) ^ 1
        direct[r] = grp[k] if k < len(grp) else None
    for r in range(n):
        c = cores[r]
        free = [h for h in range(c - topo.CORES_PER_CHIP + 1, c + topo.CORES_PER_CHIP)
                if h >= 0 and h not in cores and topo.host(h) == topo.host(c) and topo.chip(h) == topo.chip(c)]
        rest = [q for q in range(n) if q != r and q != direct[r]]
        rest.sort(key=lambda q: (sum(1 for h in free if topo.may_write(h, cores[q])), q))
        out = {}
        for q in rest:
            kind = topo.same_plane(c, cores[q])
            h = min([h for h in free if topo.may_write(h, cores[q])],
                    key=lambda h: (out.get((kind, topo.die(h)), 0), load.get((q, topo.die(h)), 0),
                                   sum(1 for p in cores if topo.may_write(h, p)), h))
            free.remove(h)
            relay[(r, q)] = h
            load[(q, topo.die(h))] = load.get((q, topo.die(h)), 0) + 1
            out[(kind, topo.die(h))] = out.get((kind, topo.die(h)), 0) + 1
    return direct, relay


def _teams(relay, cores, topo):
    state, teams = {}, {}
    for r in range(len(cores)):
        own = topo.die(cores[r])
        mine = sorted((q, h) for (rr, q), h in relay.items() if rr == r)
        rank_of = {}
        for t in mine:
            seen = state.get((t[0], topo.die(t[1])), [])
            want = 1 if not seen else (2 if any(seen) else 0)
            rank_of[t] = (want, topo.same_plane(cores[r], cores[t[0]]), topo.die(t[1]) == own, t)
        ranked = sorted(mine, key=lambda t: rank_of[t])
        half = (len(mine) + 1) // 2
        early = []
        for t in ranked:
            if len(early) < half and 2 * sum(1 for u in early if topo.die(u[1]) == topo.die(t[1])) < half:
                early.append(t)
        for t in ranked:
            if len(early) < half and t not in early:
                early.append(t)
        late = [t for t in mine if t not in early]
        teams[r] = (sorted(early, key=lambda t: (topo.die(t[1]) == own, rank_of[t]))
                    + sorted(late, key=lambda t: (topo.die(t[1]) == own, rank_of[t])))
        for t in mine:
            state.setdefault((t[0], topo.die(t[1])), []).append(t in early)
    return teams


def _share(direct, teams, r):
    peers = [p for p in sorted(direct) if direct[p] == r]
    return teams[r], peers, len(teams[r]) + len(peers) + 1


def _per(team, core, topo):
    on = _bits(topo.mask(core, team[0][1]))
    per = 1
    while per * 2 * len(team) <= len(on):
        per *= 2
    return on, per


def _engines(team, core, far, topo):
    on, per = _per(team, core, topo)
    off = 0 if far is None else topo.mask(core, far)
    on = [b for b in on if (off >> b) & 1] + [b for b in on if not (off >> b) & 1]
    nh = (len(team) + 1) // 2
    nl = len(team) - nh
    a, b = on[:per * nh], on[per * nh:per * len(team)]
    return [a[i::nh] for i in range(nh)] + [b[i::nl] for i in range(nl)]


def _block(i, k):
    u = CW // 8
    return (u * i // k) * 8, (u * (i + 1) // k) * 8


def _cmask(h, own, dst, topo):
    return topo.mask(h, dst) & topo.mask(h, own)


def _slot(T, j):
    return T.wall[:, j * P:(j + 1) * P]


def _helper(g, core, T, topo, direct, teams, r, q):
    S = T.sem
    cores = list(T.cores)
    own, dst = cores[r], cores[q]
    team, _, k = _share(direct, teams, r)
    a, b = _block(len(team) - 1 - team.index((q, core)), k)
    g.vector.memset(T.cst[:, a:b], 1.0).then_inc(S.c_fill, 1)
    g.wait_ge(S.c_fill, 1)
    if a < TK:
        e = min(b, TK)
        g.affine_select(T.cst[:, a:e], T.cst[:, a:e], [[-1, e - a]], AluOpType.is_equal, 0.0, -a, 1).then_inc(S.c_sel, 1)
        g.wait_ge(S.c_sel, 1)
    mc = _cmask(core, own, dst, topo)
    rid, pid = topo.addr(own, core)
    g.remote_dma(T.cst[:, a:b], T.cst[:, a:b], S.c_cst, S.sent, pid, rid, mc)

    g.wait_ge(S.hop, _per(team, own, topo)[1])
    rid, pid = topo.addr(dst, core)
    m = topo.mask(core, dst)
    g.remote_dma(_slot(T, r), T.wd[:], S["arr%d" % r], S.sent, pid, rid, m)
    g.wait_ge(S.sent, len(_bits(mc)) + len(_bits(m)))


def rank_program(g, core, T, topo):
    cores = list(T.cores)
    direct, relay = _plan(cores, topo)
    teams = _teams(relay, cores, topo)
    rank = T.rank_of(core)
    if rank is None:
        for (r, q), h in relay.items():
            if h == core:
                _helper(g, core, T, topo, direct, teams, r, q)
        return
    S = T.sem
    H = TK
    ident, ones = T.cst[0:H, 0:TK], T.cst[0:H, TK:CW]
    team, peers, k = _share(direct, teams, rank)
    n_cst = sum(len(_bits(_cmask(h, core, cores[q], topo))) for q, h in team)
    n_peer = sum(len(_bits(topo.mask(cores[p], core))) for p in peers)
    far = direct[rank]

    g.sync.dma_start(T.wd[:], T.w[:]).then_inc(S.ld_wd, 16)
    g.scalar.dma_start(T.xs[:], T.x[:]).then_inc(S.ld_xr, 16)
    g.sync.dma_start(T.rts[:], T.rt[:]).then_inc(S.ld_xr, 16)

    sent = 0
    if far is not None:
        tq, pq, kq = _share(direct, teams, far)
        a1, b1 = _block(len(tq) + pq.index(rank), kq)
        g.vector.memset(T.ob[:, 0:b1 - a1], 1.0).then_inc(S.c_own, 1)
        g.wait_ge(S.c_own, 1)
        rid, pid = topo.addr(cores[far], core)
        m = topo.mask(core, cores[far])
        g.remote_dma(T.cst[:, a1:b1], T.ob[:, 0:b1 - a1], S.c_peer, S.sent, pid, rid, m)
        sent += len(_bits(m))
    a0, b0 = _block(k - 1, k)
    g.vector.memset(T.zb[0:H, 0:b0 - a0], 0.0).then_inc(S.c_zero, 1)
    g.scalar.wait_ge(S.c_zero, 1)
    g.scalar.activation(T.cst[0:H, a0:b0], T.zb[0:H, 0:b0 - a0], ActivationFunctionType.Exp).then_inc(S.a_one, 1)

    g.wait_ge(S.ld_wd, 16)
    per = _per(team, core, topo)[1]
    eng = _engines(team, core, None if far is None else cores[far], topo)
    trs = []
    for i, (q, h) in enumerate(team):
        rid, pid = topo.addr(h, core)
        trs.append(RemoteDMATransfer(dst_ids=[DstId(rid=rid, pnc=pid)], dma_engine_mask=_mask(eng[i]),
                                     remote_sem=S.hop, src=T.wd[:], dst=T.wd[:]))
    g.remote_dma_fused(trs, local_sem=S.sent1)
    if far is not None:
        rid, pid = topo.addr(cores[far], core)
        m = topo.mask(core, cores[far])
        g.remote_dma(_slot(T, rank), T.wd[:], S["arr%d" % rank], S.sent, pid, rid, m)
        sent += len(_bits(m))

    g.sync.wait_ge(S.sent1, per * len(team))
    g.sync.dma_start(_slot(T, rank), T.w[:]).then_inc(S.ld_ws, 16)

    g.tensor.wait_ge(S.ld_xr, 32)
    g.tensor.matmul(T.ps_s[0:H, 0:N], T.xs[:], T.rts[:], True, True).then_inc(S.m_s, 1)
    g.vector.wait_ge(S.m_s, 1)
    g.vector.tensor_reduce(T.negm[0:H, :], T.ps_s[0:H, 0:N], AxisListType.X, AluOpType.max, negate=True).then_inc(S.v_max, 1)
    g.scalar.wait_ge(S.v_max, 1)
    g.scalar.activation(T.e[0:H, :], T.ps_s[0:H, 0:N], ActivationFunctionType.Exp, bias=T.negm[0:H, :], scale=1.0,
                        accum_out=T.ssum[0:H, :]).then_inc(S.a_exp, 1)
    g.vector.wait_ge(S.a_exp, 1)
    g.vector.wait_ge(S.c_cst, n_cst)
    for j in range(N):
        g.vector.tensor_scalar(T.dg[0:H, j * TK:(j + 1) * TK], ident, T.e[0:H, j:j + 1], None,
                               AluOpType.mult).then_inc(S.v_dg, 1)
    g.vector.reciprocal(T.rinv[0:H, :], T.ssum[0:H, :]).then_inc(S.v_rcp, 1)
    g.vector.wait_ge(S.v_rcp, 1)
    g.vector.tensor_scalar(T.dr[0:H, :], ident, T.rinv[0:H, :], None, AluOpType.mult).then_inc(S.v_dr, 1)
    g.tensor.wait_ge(S.v_dg, N)
    g.tensor.wait_ge(S.c_cst, n_cst)
    g.tensor.wait_ge(S.a_one, 1)
    if n_peer:
        g.tensor.wait_ge(S.c_peer, n_peer)
    g.tensor.matmul(T.ps_g[:, 0:N * TK], ones, T.dg[0:H, :], True, True).then_inc(S.m_g, 1)
    g.tensor.wait_ge(S.v_dr, 1)
    g.tensor.matmul(T.ps_r[:, 0:TK], ones, T.dr[0:H, :], True, True).then_inc(S.m_r, 1)
    g.vector.wait_ge(S.m_g, 1)
    g.vector.wait_ge(S.ld_xr, 32)
    for j in range(N):
        b = slice(j * TK, (j + 1) * TK)
        g.vector.tensor_tensor(T.xg[:, b], T.ps_g[:, b], T.xs[:], AluOpType.mult).then_inc(S.v_xg, 1)
    g.vector.wait_ge(S.m_r, 1)
    g.vector.tensor_copy(T.rb[:], T.ps_r[:, 0:TK]).then_inc(S.v_rb, 1)

    g.tensor.wait_ge(S.v_xg, N)
    others = [j for j in range(N) if j != rank]
    others.sort(key=lambda j: (0, 0, 0, j) if direct[j] == rank else
                (1, teams[j].index((rank, relay[(j, rank)])), not topo.same_plane(cores[j], core), j))
    for i, j in enumerate([rank] + others):
        if j == rank:
            g.tensor.wait_ge(S.ld_ws, 16)
        else:
            src = cores[j] if direct[j] == rank else relay[(j, rank)]
            g.tensor.wait_ge(S["arr%d" % j], len(_bits(topo.mask(src, core))))
        mm = g.tensor.matmul(T.ps_y[:, 0:TK], _slot(T, j), T.xg[:, j * TK:(j + 1) * TK], i == 0, i == N - 1)
    mm.then_inc(S.m_y, 1)
    g.vector.wait_ge(S.v_rb, 1)
    g.vector.wait_ge(S.m_y, 1)
    g.vector.tensor_tensor(T.ysb[:], T.ps_y[:, 0:TK], T.rb[:], AluOpType.mult).then_inc(S.v_y, 1)
    g.sync.wait_ge(S.v_y, 1)
    g.sync.dma_start(T.y[:], T.ysb[:]).then_inc(S.st_y, 16)
    g.sync.wait_ge(S.st_y, 16)
    g.wait_ge(S.sent1, per * len(team))
    g.wait_ge(S.sent, sent)
